import numpy as np
import ml_dtypes


def mxq(x, axis, fmt="e4m3"):
    dtype, down = {"e4m3": (ml_dtypes.float8_e4m3fn, 7), "e5m2": (ml_dtypes.float8_e5m2, 14)}[fmt]
    v = np.moveaxis(np.asarray(x, np.float32).astype(ml_dtypes.bfloat16).astype(np.float64), axis, -1)
    blocks = v.reshape(v.shape[:-1] + (-1, 32))
    amax = np.abs(blocks).max(-1, keepdims=True)
    byte = np.maximum(np.where(amax > 0, np.frexp(amax)[1] - 1 + 127, 0) - down, 1)
    scale = np.exp2(byte - 127.0)
    codes = (blocks / scale).astype(np.float32).astype(dtype).astype(np.float64)
    return np.moveaxis((codes * scale).reshape(v.shape), -1, axis)


WIDE = False


def mx_kscale(k):
    if not WIDE:
        return np.ones(k)
    levels = np.array([24, -24, 12, -12, 0])
    if k % 512:
        return np.exp2(np.random.permutation(np.resize(levels, k // 32))).repeat(32)
    a = np.empty((k // 512, 16))
    for p in range(k // 512):
        a[p, :8] = np.random.permutation(np.resize(levels, 8))
        for g in range(8):
            far = levels[np.abs(levels - a[p, g]) >= 10]
            a[p, g + 8] = far[np.random.randint(len(far))]
    return np.exp2(a.ravel()).repeat(32)


def f64(x):
    return np.asarray(x).astype(np.float64)


E2M1 = np.array([0.0, 0.5, 1.0, 1.5, 2.0, 3.0, 4.0, 6.0, -0.0, -0.5, -1.0, -1.5, -2.0, -3.0, -4.0, -6.0])


def pack_weight(w, fmt):
    k, n = w.shape
    w = f64(np.asarray(w, np.float32).astype(ml_dtypes.bfloat16)).reshape(k // 32, 32, n)
    amax = np.abs(w).max(1)
    if fmt == "e4m3":
        byte = np.frexp(amax)[1] - 1 + 127 - 7
    else:
        mant, ex = np.frexp(amax / 6.0)
        byte = np.where(mant > 0.5, ex, ex - 1) + 127
    byte = np.clip(np.where(amax > 0, byte, 1), 1, 254)
    scaled = (w * np.exp2(127.0 - byte)[:, None, :]).reshape(k, n).astype(np.float32)
    by_word = np.ascontiguousarray(scaled.reshape(k // 512, 128, 4, n).transpose(0, 1, 3, 2))
    if fmt == "e4m3":
        words = by_word.astype(ml_dtypes.float8_e4m3fn).view(np.uint8)
    else:
        c = by_word.astype(ml_dtypes.float4_e2m1fn).view(np.uint8) & 0xF
        words = (c[..., 0::2] | (c[..., 1::2] << 4)).reshape(k // 512, 128, 2 * n)
    return np.ascontiguousarray(words), np.ascontiguousarray(byte.astype(np.uint8).reshape(k // 512, 16, n))


def unpack_weight(words, scales, fmt):
    g, _, n = scales.shape
    words = np.ascontiguousarray(words).reshape(g, 128, n, -1)
    if fmt == "e4m3":
        vals = words.view(ml_dtypes.float8_e4m3fn).astype(np.float64)
    else:
        nib = np.empty((g, 128, n, 4), np.uint8)
        nib[..., 0::2] = words & 0xF
        nib[..., 1::2] = words >> 4
        vals = E2M1[nib]
    vals = vals * np.repeat(np.exp2(scales.astype(np.float64) - 127.0), 8, axis=1)[..., None]
    return vals.transpose(0, 1, 3, 2).reshape(g * 512, n)


K, R, N, T = 1024, 512, 512, 512


def setup_inputs():
    n = np.random.standard_normal
    s = mx_kscale(K)[:, None]
    u = mx_kscale(R)[:, None]
    p_wb = pack_weight(0.7 * n((K, N)) / np.sqrt(K) / s, "e4m3")
    return {
        "x": (n((K, T)) * s).astype(np.float32),
        "wb_words": p_wb[0],
        "wb_scales": p_wb[1],
        "dn": (n((K, R)) / np.sqrt(K) / s * u.T).astype(np.float32),
        "upw": (n((R, N)) / np.sqrt(R) / u).astype(np.float32),
        "x0": (n((N, T))).astype(np.float32),
        "b": (0.3 * n(N)).astype(np.float32),
        "xr": (n((N, T))).astype(np.float32),
    }


def reference(x, wb_words, wb_scales, dn, upw, x0, b, xr):
    x_ = mxq(f64(x), 0, "e4m3")
    wb_ = unpack_weight(wb_words, wb_scales, "e4m3")
    dn_ = mxq(f64(dn), 0, "e4m3")
    upw_ = mxq(f64(upw), 0, "e4m3")
    hs = dn_.T @ x_
    h_ = mxq(hs, 0, "e4m3")
    y = wb_.T @ x_ + upw_.T @ h_
    return f64(x0) * (y + f64(b)[:, None]) + f64(xr)

@@ -1,0 +1,216 @@
+from contextlib import ExitStack
+
+import concourse.mybir as mybir
+from concourse.masks import make_identity
+
+K, R, N, T = 1024, 512, 512, 512
+FLOPS = 2 * T * (K * R + K * N + R * N)
+
+F32 = mybir.dt.float32
+BF16 = mybir.dt.bfloat16
+I32 = mybir.dt.int32
+U32 = mybir.dt.uint32
+U8 = mybir.dt.uint8
+FP8X4 = mybir.dt.float8_e4m3fn_x4
+ADD = mybir.AluOpType.add
+MULT = mybir.AluOpType.mult
+
+P = 128
+PACK = 4
+K_PASS = P * PACK
+PASSES = K // K_PASS
+TILES = 4
+LINE = 4
+
+
+def tile_mix_cross_none_kernel(tc, x, wb_words, wb_scales, dn, upw, x0, b, xr, out):
+    nc = tc.nc
+
+    with ExitStack() as ctx:
+        sb = ctx.enter_context(tc.tile_pool(name="sb", bufs=1))
+        ps = ctx.enter_context(tc.psum_pool(name="ps", bufs=1))
+        ctx.enter_context(tc.manual_schedule())
+
+        def sbuf(name, shape, dtype):
+            return sb.tile(shape, dtype, name=name, align_bytes=64)
+
+        def operand(name):
+            return sbuf(name + "_codes", [P, 512], U32), sbuf(name + "_scales", [P, 512], U8)
+
+        def load_rows(name, rows):
+            raw = sbuf(name, [P, PACK, rows.shape[1]], F32)
+            nc.sync.dma_start(out=raw[:], in_=rows.rearrange("(p k) w -> p k w", k=PACK))
+            return raw
+
+        def load_tile(name, src, c):
+            t = sbuf(name, [P, T], F32)
+            nc.sync.dma_start(out=t[:], in_=src[c * P : (c + 1) * P, :])
+            return t
+
+        def load_wb(a):
+            words = sbuf("wb_codes%d" % a, [P, N], U32)
+            nc.sync.dma_start(out=words[:].bitcast(I32), in_=wb_words[a].rearrange("p n i -> p (n i)").bitcast(I32))
+            return words
+
+        def copy_on(engine, dst, src):
+            if engine == "vector":
+                nc.vector.tensor_copy(out=dst, in_=src)
+            else:
+                nc.scalar.copy(out=dst, in_=src)
+
+        def interleave(engine, name, raw, lo, width):
+            grouped = sbuf(name, [P, width, PACK], BF16)
+            copy_on(
+                engine,
+                grouped[:].rearrange("p (c i) k -> p c k i", i=LINE),
+                raw[:, :, lo : lo + width].rearrange("p k (c i) -> p c k i", i=LINE),
+            )
+            return grouped
+
+        def interleave_dn(engine, name, raw, j0):
+            grouped = sbuf(name, [P, 2 * P, PACK], BF16)
+            copy_on(
+                engine,
+                grouped[:].rearrange("p (j m) k -> p m k j", j=2),
+                raw[:].rearrange("p k (m j) -> p m k j", j=PACK)[:, :, :, j0 : j0 + 2],
+            )
+            return grouped
+
+        def quantize(dst, lo, grouped):
+            codes, scales = dst
+            width = grouped.shape[1]
+            nc.vector.quantize_mx(
+                out=codes[:, lo : lo + width].bitcast(FP8X4),
+                scales=scales[:, lo : lo + width],
+                in_=grouped[:].rearrange("p w k -> p (w k)"),
+            )
+
+        def mx(acc, lhs, lhs_lo, rhs, rhs_lo, width, start, stop):
+            nc.tensor.matmul_mx(
+                out=acc,
+                lhsT=lhs[0][:, lhs_lo : lhs_lo + P].bitcast(FP8X4),
+                lhsT_scale=lhs[1][:, lhs_lo : lhs_lo + P],
+                rhs=rhs[0][:, rhs_lo : rhs_lo + width].bitcast(FP8X4),
+                rhs_scale=rhs[1][:, rhs_lo : rhs_lo + width],
+                start=start,
+                stop=stop,
+            )
+
+        half = T // 2
+        dn_raw0 = load_rows("dn_raw0", dn[0:K_PASS, :])
+        x_raw0 = load_rows("x_raw0", x[0:K_PASS, :])
+        dn_raw1 = load_rows("dn_raw1", dn[K_PASS:K, :])
+        wb_plane = sbuf("wb_plane", [P, PASSES, N], U8)
+        b_rows = sbuf("b_rows", [P, P], F32)
+        nc.vector.memset(wb_plane[:].bitcast(I32), 0)
+        nc.vector.memset(b_rows[:], 0.0)
+        scale_words = wb_scales.bitcast(I32)
+        for q in range(4):
+            nc.scalar.dma_start(
+                out=wb_plane[32 * q : 32 * q + 4, :, :].bitcast(I32),
+                in_=scale_words[:, 4 * q : 4 * q + 4, :].rearrange("a r n -> r a n"),
+            )
+        nc.scalar.dma_start(out=b_rows[0:TILES, :], in_=b.rearrange("(c p) -> c p", p=P))
+        x_raw1a = load_rows("x_raw1a", x[K_PASS:K, 0:half])
+        x_raw1b = load_rows("x_raw1b", x[K_PASS:K, half:T])
+        wb_codes0 = load_wb(0)
+        up_raw = load_rows("up_raw", upw)
+        wb_codes1 = load_wb(1)
+        x0_t = [None] * TILES
+        xr_t = [None] * TILES
+        x0_t[0] = load_tile("x0_0", x0, 0)
+        for c in range(1, TILES):
+            x0_t[c] = load_tile("x0_%d" % c, x0, c)
+            xr_t[c - 1] = load_tile("xr_%d" % (c - 1), xr, c - 1)
+        xr_t[TILES - 1] = load_tile("xr_%d" % (TILES - 1), xr, TILES - 1)
+
+        wb = [(wb_codes0, wb_plane[:, 0, :]), (wb_codes1, wb_plane[:, 1, :])]
+        ident = sbuf("ident", [P, P], F32)
+        make_identity(nc, ident[:])
+
+        hs = [ps.tile([P, PACK, P], F32, name="hs%d" % q) for q in range(TILES)]
+        y = [ps.tile([P, T], F32, name="y%d" % c) for c in range(TILES)]
+
+        dn_q = [operand("dn0"), operand("dn1")]
+        x_q = [operand("x0q"), operand("x1q")]
+        up_q = operand("up")
+        h_q = operand("h")
+
+        def prepare_dn(a, raw):
+            lo = interleave_dn("vector", "dn_lo%d" % a, raw, 0)
+            hi = interleave_dn("scalar", "dn_hi%d" % a, raw, 2)
+            quantize(dn_q[a], 0, lo)
+            quantize(dn_q[a], 2 * P, hi)
+
+        def prepare_x(a, name, raw, base, width):
+            lo = interleave("vector", name + "_lo", raw, 0, width)
+            hi = interleave("scalar", name + "_hi", raw, width, width)
+            quantize(x_q[a], base, lo)
+            quantize(x_q[a], base + width, hi)
+
+        def hs_pass(a, q):
+            for j in range(PACK):
+                mx(hs[q][:, j, :], dn_q[a], j * P, x_q[a], q * P, P,
+                   start=(a == 0 and j == 0), stop=(a == PASSES - 1 and j == PACK - 1))
+
+        prepare_dn(0, dn_raw0)
+        prepare_x(0, "xg0", x_raw0, 0, half)
+
+        b_cols = sbuf("b_cols", [P, TILES], F32)
+        nc.tensor.transpose(y[TILES - 1][:, 0:P], b_rows[:], ident[:])
+        nc.scalar.copy(out=b_cols[:], in_=y[TILES - 1][:, 0:TILES])
+
+        for q in range(TILES):
+            hs_pass(0, q)
+        prepare_dn(1, dn_raw1)
+        prepare_x(1, "xg1a", x_raw1a, 0, P)
+        prepare_x(1, "xg1b", x_raw1b, half, P)
+        for q in range(TILES):
+            hs_pass(1, q)
+
+        h_grouped = [sbuf("hg0", [P, half, PACK], BF16), sbuf("hg1", [P, half, PACK], BF16)]
+        for q in range(TILES):
+            copy_on(
+                "scalar" if q % 2 == 0 else "vector",
+                h_grouped[q // 2][:, (q % 2) * P : (q % 2 + 1) * P, :],
+                hs[q][:].rearrange("p j t -> p t j"),
+            )
+        quantize(h_q, 0, h_grouped[0])
+        quantize(h_q, half, h_grouped[1])
+
+        for c in range(TILES):
+            mx(y[c][:], wb[0], c * P, x_q[0], 0, T, start=True, stop=False)
+
+        up_g = [interleave("vector" if c == 0 else "scalar", "upg%d" % c, up_raw, c * P, P) for c in range(TILES)]
+
+        z = sbuf("z", [P, TILES, T], F32)
+        out_v = out.rearrange("(c p) t -> p c t", p=P)
+
+        def finish_y(c):
+            quantize(up_q, c * P, up_g[c])
+            mx(y[c][:], wb[1], c * P, x_q[1], 0, T, start=False, stop=False)
+            mx(y[c][:], up_q, c * P, h_q, 0, T, start=False, stop=True)
+
+        def scale(c):
+            nc.vector.scalar_tensor_tensor(
+                out=z[:, c, :], in0=y[c][:], scalar=b_cols[:, c : c + 1], in1=x0_t[c][:], op0=ADD, op1=MULT
+            )
+
+        def residual(c):
+            nc.vector.tensor_tensor(out=z[:, c, :], in0=z[:, c, :], in1=xr_t[c][:], op=ADD)
+
+        finish_y(0)
+        finish_y(1)
+        scale(0)
+        finish_y(2)
+        scale(1)
+        finish_y(3)
+        residual(0)
+        scale(2)
+        residual(1)
+        nc.sync.dma_start(out=out_v[:, 0:2, :], in_=z[:, 0:2, :])
+        scale(3)
+        residual(2)
+        nc.sync.dma_start(out=out_v[:, 2, :], in_=z[:, 2, :])
+        residual(3)
+        nc.sync.dma_start(out=out_v[:, 3, :], in_=z[:, 3, :])

@@ -47,11 +47,6 @@ def tile_mix_cross_none_kernel(tc, x, wb_words, wb_scales, dn, upw, x0, b, xr, o
             nc.sync.dma_start(out=t[:], in_=src[c * P : (c + 1) * P, :])
             return t
 
-        def load_wb(a):
-            words = sbuf("wb_codes%d" % a, [P, N], U32)
-            nc.sync.dma_start(out=words[:].bitcast(I32), in_=wb_words[a].rearrange("p n i -> p (n i)").bitcast(I32))
-            return words
-
         def copy_on(engine, dst, src):
             if engine == "vector":
                 nc.vector.tensor_copy(out=dst, in_=src)
@@ -98,33 +93,31 @@ def tile_mix_cross_none_kernel(tc, x, wb_words, wb_scales, dn, upw, x0, b, xr, o
 
         half = T // 2
         dn_raw0 = load_rows("dn_raw0", dn[0:K_PASS, :])
-        x_raw0 = load_rows("x_raw0", x[0:K_PASS, :])
         dn_raw1 = load_rows("dn_raw1", dn[K_PASS:K, :])
-        wb_plane = sbuf("wb_plane", [P, PASSES, N], U8)
+        x_raw0 = load_rows("x_raw0", x[0:K_PASS, :])
+        x_raw1 = load_rows("x_raw1", x[K_PASS:K, :])
+        wb_plane = sbuf("wb_plane", [P, N], U8)
         b_rows = sbuf("b_rows", [P, P], F32)
         nc.vector.memset(wb_plane[:].bitcast(I32), 0)
         nc.vector.memset(b_rows[:], 0.0)
         scale_words = wb_scales.bitcast(I32)
         for q in range(4):
-            nc.scalar.dma_start(
-                out=wb_plane[32 * q : 32 * q + 4, :, :].bitcast(I32),
-                in_=scale_words[:, 4 * q : 4 * q + 4, :].rearrange("a r n -> r a n"),
+            nc.sync.dma_start(
+                out=wb_plane[32 * q : 32 * q + 8, :].bitcast(I32),
+                in_=scale_words[:, 4 * q : 4 * q + 4, :],
             )
-        nc.scalar.dma_start(out=b_rows[0:TILES, :], in_=b.rearrange("(c p) -> c p", p=P))
-        x_raw1a = load_rows("x_raw1a", x[K_PASS:K, 0:half])
-        x_raw1b = load_rows("x_raw1b", x[K_PASS:K, half:T])
-        wb_codes0 = load_wb(0)
+        nc.sync.dma_start(out=b_rows[0:TILES, :], in_=b.rearrange("(c p) -> c p", p=P))
         up_raw = load_rows("up_raw", upw)
-        wb_codes1 = load_wb(1)
-        x0_t = [None] * TILES
-        xr_t = [None] * TILES
-        x0_t[0] = load_tile("x0_0", x0, 0)
+        wb_codes = sbuf("wb_codes", [P, PASSES, N], U32)
+        nc.sync.dma_start(out=wb_codes[:].bitcast(I32), in_=wb_words.rearrange("a p n i -> p a (n i)").bitcast(I32))
+        x0_t = [load_tile("x0_0", x0, 0)]
+        xr_t = []
         for c in range(1, TILES):
-            x0_t[c] = load_tile("x0_%d" % c, x0, c)
-            xr_t[c - 1] = load_tile("xr_%d" % (c - 1), xr, c - 1)
-        xr_t[TILES - 1] = load_tile("xr_%d" % (TILES - 1), xr, TILES - 1)
+            x0_t.append(load_tile("x0_%d" % c, x0, c))
+            xr_t.append(load_tile("xr_%d" % (c - 1), xr, c - 1))
+        xr_t.append(load_tile("xr_%d" % (TILES - 1), xr, TILES - 1))
 
-        wb = [(wb_codes0, wb_plane[:, 0, :]), (wb_codes1, wb_plane[:, 1, :])]
+        wb = [(wb_codes[:, a, :], wb_plane[4 * a : P, :]) for a in range(PASSES)]
         ident = sbuf("ident", [P, P], F32)
         make_identity(nc, ident[:])
 
@@ -142,11 +135,15 @@ def tile_mix_cross_none_kernel(tc, x, wb_words, wb_scales, dn, upw, x0, b, xr, o
             quantize(dn_q[a], 0, lo)
             quantize(dn_q[a], 2 * P, hi)
 
-        def prepare_x(a, name, raw, base, width):
-            lo = interleave("vector", name + "_lo", raw, 0, width)
-            hi = interleave("scalar", name + "_hi", raw, width, width)
-            quantize(x_q[a], base, lo)
-            quantize(x_q[a], base + width, hi)
+        def prepare_x(a, raw):
+            g0 = interleave("vector", "xg%d_0" % a, raw, 0, P)
+            g1 = interleave("scalar", "xg%d_1" % a, raw, P, P)
+            g2 = interleave("vector", "xg%d_2" % a, raw, 2 * P, P)
+            quantize(x_q[a], 0, g0)
+            g3 = interleave("vector", "xg%d_3" % a, raw, 3 * P, P)
+            quantize(x_q[a], P, g1)
+            quantize(x_q[a], 2 * P, g2)
+            quantize(x_q[a], 3 * P, g3)
 
         def hs_pass(a, q):
             for j in range(PACK):
@@ -154,63 +151,73 @@ def tile_mix_cross_none_kernel(tc, x, wb_words, wb_scales, dn, upw, x0, b, xr, o
                    start=(a == 0 and j == 0), stop=(a == PASSES - 1 and j == PACK - 1))
 
         prepare_dn(0, dn_raw0)
-        prepare_x(0, "xg0", x_raw0, 0, half)
-
-        b_cols = sbuf("b_cols", [P, TILES], F32)
+        prepare_dn(1, dn_raw1)
+        for a, raw in enumerate((x_raw0, x_raw1)):
+            prepare_x(a, raw)
+            for q in range(TILES):
+                hs_pass(a, q)
         nc.tensor.transpose(y[TILES - 1][:, 0:P], b_rows[:], ident[:])
+
+        h01 = sbuf("h01", [P, half, PACK], BF16)
+        h2 = sbuf("h2", [P, P, PACK], BF16)
+        h3 = sbuf("h3", [P, P, PACK], BF16)
+
+        def drain_h(engine, q, dst):
+            copy_on(engine, dst, hs[q][:].rearrange("p j t -> p t j"))
+
+        drain_h("scalar", 0, h01[:, 0:P, :])
+        drain_h("vector", 1, h01[:, P:half, :])
+        drain_h("scalar", 2, h2[:])
+        drain_h("scalar", 3, h3[:])
+        b_cols = sbuf("b_cols", [P, TILES], F32)
         nc.scalar.copy(out=b_cols[:], in_=y[TILES - 1][:, 0:TILES])
 
-        for q in range(TILES):
-            hs_pass(0, q)
-        prepare_dn(1, dn_raw1)
-        prepare_x(1, "xg1a", x_raw1a, 0, P)
-        prepare_x(1, "xg1b", x_raw1b, half, P)
-        for q in range(TILES):
-            hs_pass(1, q)
+        up_g0 = interleave("vector", "up_g0", up_raw, 0, P)
+        quantize(h_q, 0, h01)
+        quantize(up_q, 0, up_g0)
+        quantize(h_q, 2 * P, h2)
+        quantize(h_q, 3 * P, h3)
+        up_g1 = interleave("vector", "up_g1", up_raw, P, P)
+        up_g2 = interleave("scalar", "up_g2", up_raw, 2 * P, P)
+        up_g3 = interleave("scalar", "up_g3", up_raw, 3 * P, P)
+        quantize(up_q, 2 * P, up_g2)
+        quantize(up_q, P, up_g1)
 
-        h_grouped = [sbuf("hg0", [P, half, PACK], BF16), sbuf("hg1", [P, half, PACK], BF16)]
-        for q in range(TILES):
-            copy_on(
-                "scalar" if q % 2 == 0 else "vector",
-                h_grouped[q // 2][:, (q % 2) * P : (q % 2 + 1) * P, :],
-                hs[q][:].rearrange("p j t -> p t j"),
-            )
-        quantize(h_q, 0, h_grouped[0])
-        quantize(h_q, half, h_grouped[1])
+        def base_passes(c):
+            for a in range(PASSES):
+                mx(y[c][:], wb[a], c * P, x_q[a], 0, T, start=(a == 0), stop=False)
 
-        for c in range(TILES):
-            mx(y[c][:], wb[0], c * P, x_q[0], 0, T, start=True, stop=False)
-
-        up_g = [interleave("vector" if c == 0 else "scalar", "upg%d" % c, up_raw, c * P, P) for c in range(TILES)]
+        def branch_pass(c, t0, width):
+            mx(y[c][:, t0 : t0 + width], up_q, c * P, h_q, t0, width, start=False, stop=(t0 + width == T))
 
         z = sbuf("z", [P, TILES, T], F32)
-        out_v = out.rearrange("(c p) t -> p c t", p=P)
-
-        def finish_y(c):
-            quantize(up_q, c * P, up_g[c])
-            mx(y[c][:], wb[1], c * P, x_q[1], 0, T, start=False, stop=False)
-            mx(y[c][:], up_q, c * P, h_q, 0, T, start=False, stop=True)
 
         def scale(c):
             nc.vector.scalar_tensor_tensor(
                 out=z[:, c, :], in0=y[c][:], scalar=b_cols[:, c : c + 1], in1=x0_t[c][:], op0=ADD, op1=MULT
             )
 
-        def residual(c):
-            nc.vector.tensor_tensor(out=z[:, c, :], in0=z[:, c, :], in1=xr_t[c][:], op=ADD)
+        def finish(c, t0, width):
+            cols = slice(t0, t0 + width)
+            nc.vector.tensor_tensor(out=z[:, c, cols], in0=z[:, c, cols], in1=xr_t[c][:, cols], op=ADD)
+            nc.sync.dma_start(out=out[c * P : (c + 1) * P, cols], in_=z[:, c, cols])
 
-        finish_y(0)
-        finish_y(1)
+        base_passes(0)
+        branch_pass(0, 0, half)
+        branch_pass(0, half, half)
+        base_passes(1)
+        branch_pass(1, 0, T)
+        base_passes(2)
+        branch_pass(2, 0, T)
         scale(0)
-        finish_y(2)
+        quantize(up_q, 3 * P, up_g3)
+        base_passes(3)
+        branch_pass(3, 0, T)
         scale(1)
-        finish_y(3)
-        residual(0)
+        finish(0, 0, T)
         scale(2)
-        residual(1)
-        nc.sync.dma_start(out=out_v[:, 0:2, :], in_=z[:, 0:2, :])
+        finish(1, 0, T)
         scale(3)
-        residual(2)
-        nc.sync.dma_start(out=out_v[:, 2, :], in_=z[:, 2, :])
-        residual(3)
-        nc.sync.dma_start(out=out_v[:, 3, :], in_=z[:, 3, :])
+        finish(2, 0, T)
+        finish(3, 0, half)
+        finish(3, half, half)

@@ -42,10 +42,15 @@ def tile_mix_cross_none_kernel(tc, x, wb_words, wb_scales, dn, upw, x0, b, xr, o
             nc.sync.dma_start(out=raw[:], in_=rows.rearrange("(p k) w -> p k w", k=PACK))
             return raw
 
-        def load_tile(name, src, c):
-            t = sbuf(name, [P, T], F32)
-            nc.sync.dma_start(out=t[:], in_=src[c * P : (c + 1) * P, :])
+        def load_tile(name, src, c, t0, width):
+            t = sbuf(name, [P, width], F32)
+            nc.sync.dma_start(out=t[:], in_=src[c * P : (c + 1) * P, t0 : t0 + width])
             return t
+
+        def load_wb(a):
+            words = sbuf("wb_codes%d" % a, [P, N], U32)
+            nc.sync.dma_start(out=words[:].bitcast(I32), in_=wb_words[a].rearrange("p n i -> p (n i)").bitcast(I32))
+            return words
 
         def copy_on(engine, dst, src):
             if engine == "vector":
@@ -93,31 +98,32 @@ def tile_mix_cross_none_kernel(tc, x, wb_words, wb_scales, dn, upw, x0, b, xr, o
 
         half = T // 2
         dn_raw0 = load_rows("dn_raw0", dn[0:K_PASS, :])
+        b_rows = sbuf("b_rows", [P, P], F32)
+        nc.vector.memset(b_rows[:], 0.0)
+        nc.sync.dma_start(out=b_rows[0:TILES, :], in_=b.rearrange("(c p) -> c p", p=P))
         dn_raw1 = load_rows("dn_raw1", dn[K_PASS:K, :])
         x_raw0 = load_rows("x_raw0", x[0:K_PASS, :])
         x_raw1 = load_rows("x_raw1", x[K_PASS:K, :])
         wb_plane = sbuf("wb_plane", [P, N], U8)
-        b_rows = sbuf("b_rows", [P, P], F32)
         nc.vector.memset(wb_plane[:].bitcast(I32), 0)
-        nc.vector.memset(b_rows[:], 0.0)
         scale_words = wb_scales.bitcast(I32)
         for q in range(4):
             nc.sync.dma_start(
                 out=wb_plane[32 * q : 32 * q + 8, :].bitcast(I32),
                 in_=scale_words[:, 4 * q : 4 * q + 4, :],
             )
-        nc.sync.dma_start(out=b_rows[0:TILES, :], in_=b.rearrange("(c p) -> c p", p=P))
         up_raw = load_rows("up_raw", upw)
-        wb_codes = sbuf("wb_codes", [P, PASSES, N], U32)
-        nc.sync.dma_start(out=wb_codes[:].bitcast(I32), in_=wb_words.rearrange("a p n i -> p a (n i)").bitcast(I32))
-        x0_t = [load_tile("x0_0", x0, 0)]
-        xr_t = []
-        for c in range(1, TILES):
-            x0_t.append(load_tile("x0_%d" % c, x0, c))
-            xr_t.append(load_tile("xr_%d" % (c - 1), xr, c - 1))
-        xr_t.append(load_tile("xr_%d" % (TILES - 1), xr, TILES - 1))
+        wb_codes0 = load_wb(0)
+        wb_codes1 = load_wb(1)
+        x0_t = [None] * TILES
+        xr_t = [None] * TILES
+        for name, c in (("x0", 0), ("x0", 1), ("xr", 0), ("x0", 2), ("xr", 1), ("xr", 2), ("x0", 3), ("xr", 3)):
+            if name == "x0":
+                x0_t[c] = load_tile("x0_%d" % c, x0, c, 0, T)
+            else:
+                xr_t[c] = load_tile("xr_%d" % c, xr, c, 0, T)
 
-        wb = [(wb_codes[:, a, :], wb_plane[4 * a : P, :]) for a in range(PASSES)]
+        wb = [(wb_codes0, wb_plane[0:P, :]), (wb_codes1, wb_plane[4:P, :])]
         ident = sbuf("ident", [P, P], F32)
         make_identity(nc, ident[:])
 
@@ -136,14 +142,11 @@ def tile_mix_cross_none_kernel(tc, x, wb_words, wb_scales, dn, upw, x0, b, xr, o
             quantize(dn_q[a], 2 * P, hi)
 
         def prepare_x(a, raw):
-            g0 = interleave("vector", "xg%d_0" % a, raw, 0, P)
-            g1 = interleave("scalar", "xg%d_1" % a, raw, P, P)
-            g2 = interleave("vector", "xg%d_2" % a, raw, 2 * P, P)
-            quantize(x_q[a], 0, g0)
-            g3 = interleave("vector", "xg%d_3" % a, raw, 3 * P, P)
-            quantize(x_q[a], P, g1)
-            quantize(x_q[a], 2 * P, g2)
-            quantize(x_q[a], 3 * P, g3)
+            groups = [
+                interleave("vector" if q % 2 == 0 else "scalar", "xg%d_%d" % (a, q), raw, q * P, P) for q in range(TILES)
+            ]
+            for q in range(TILES):
+                quantize(x_q[a], q * P, groups[q])
 
         def hs_pass(a, q):
             for j in range(PACK):
@@ -151,12 +154,14 @@ def tile_mix_cross_none_kernel(tc, x, wb_words, wb_scales, dn, upw, x0, b, xr, o
                    start=(a == 0 and j == 0), stop=(a == PASSES - 1 and j == PACK - 1))
 
         prepare_dn(0, dn_raw0)
+        nc.tensor.transpose(y[TILES - 1][:, 0:P], b_rows[:], ident[:])
+        b_cols = sbuf("b_cols", [P, TILES], F32)
+        nc.scalar.copy(out=b_cols[:], in_=y[TILES - 1][:, 0:TILES])
         prepare_dn(1, dn_raw1)
         for a, raw in enumerate((x_raw0, x_raw1)):
             prepare_x(a, raw)
             for q in range(TILES):
                 hs_pass(a, q)
-        nc.tensor.transpose(y[TILES - 1][:, 0:P], b_rows[:], ident[:])
 
         h01 = sbuf("h01", [P, half, PACK], BF16)
         h2 = sbuf("h2", [P, P, PACK], BF16)
@@ -169,55 +174,58 @@ def tile_mix_cross_none_kernel(tc, x, wb_words, wb_scales, dn, upw, x0, b, xr, o
         drain_h("vector", 1, h01[:, P:half, :])
         drain_h("scalar", 2, h2[:])
         drain_h("scalar", 3, h3[:])
-        b_cols = sbuf("b_cols", [P, TILES], F32)
-        nc.scalar.copy(out=b_cols[:], in_=y[TILES - 1][:, 0:TILES])
 
-        up_g0 = interleave("vector", "up_g0", up_raw, 0, P)
-        quantize(h_q, 0, h01)
-        quantize(up_q, 0, up_g0)
-        quantize(h_q, 2 * P, h2)
-        quantize(h_q, 3 * P, h3)
-        up_g1 = interleave("vector", "up_g1", up_raw, P, P)
-        up_g2 = interleave("scalar", "up_g2", up_raw, 2 * P, P)
-        up_g3 = interleave("scalar", "up_g3", up_raw, 3 * P, P)
-        quantize(up_q, 2 * P, up_g2)
-        quantize(up_q, P, up_g1)
-
-        def base_passes(c):
-            for a in range(PASSES):
-                mx(y[c][:], wb[a], c * P, x_q[a], 0, T, start=(a == 0), stop=False)
+        def base_pass(a, c):
+            mx(y[c][:], wb[a], c * P, x_q[a], 0, T, start=(a == 0), stop=False)
 
         def branch_pass(c, t0, width):
             mx(y[c][:, t0 : t0 + width], up_q, c * P, h_q, t0, width, start=False, stop=(t0 + width == T))
 
+        up_g0 = interleave("vector", "up_g0", up_raw, 0, P)
+        quantize(h_q, 0, h01)
+        quantize(up_q, 0, up_g0)
+        up_g1 = interleave("vector", "up_g1", up_raw, P, P)
+        quantize(h_q, 2 * P, h2)
+        quantize(h_q, 3 * P, h3)
+        up_g2 = interleave("scalar", "up_g2", up_raw, 2 * P, P)
+        up_g3 = interleave("scalar", "up_g3", up_raw, 3 * P, P)
+        quantize(up_q, P, up_g1)
+        quantize(up_q, 2 * P, up_g2)
+
         z = sbuf("z", [P, TILES, T], F32)
 
-        def scale(c):
+        def scale(c, t0, width):
+            cols = slice(t0, t0 + width)
             nc.vector.scalar_tensor_tensor(
-                out=z[:, c, :], in0=y[c][:], scalar=b_cols[:, c : c + 1], in1=x0_t[c][:], op0=ADD, op1=MULT
+                out=z[:, c, cols], in0=y[c][:, cols], scalar=b_cols[:, c : c + 1], in1=x0_t[c][:, cols], op0=ADD, op1=MULT
             )
 
-        def finish(c, t0, width):
+        def finish(engine, c, t0, width):
             cols = slice(t0, t0 + width)
-            nc.vector.tensor_tensor(out=z[:, c, cols], in0=z[:, c, cols], in1=xr_t[c][:, cols], op=ADD)
+            engine.tensor_tensor(out=z[:, c, cols], in0=z[:, c, cols], in1=xr_t[c][:, cols], op=ADD)
             nc.sync.dma_start(out=out[c * P : (c + 1) * P, cols], in_=z[:, c, cols])
 
-        base_passes(0)
+        base_pass(0, 0)
+        base_pass(0, 1)
+        base_pass(1, 0)
         branch_pass(0, 0, half)
         branch_pass(0, half, half)
-        base_passes(1)
+        base_pass(1, 1)
         branch_pass(1, 0, T)
-        base_passes(2)
+        base_pass(0, 2)
+        base_pass(1, 2)
         branch_pass(2, 0, T)
-        scale(0)
+        scale(0, 0, T)
         quantize(up_q, 3 * P, up_g3)
-        base_passes(3)
+        base_pass(0, 3)
+        base_pass(1, 3)
         branch_pass(3, 0, T)
-        scale(1)
-        finish(0, 0, T)
-        scale(2)
-        finish(1, 0, T)
-        scale(3)
-        finish(2, 0, T)
-        finish(3, 0, half)
-        finish(3, half, half)
+        scale(1, 0, T)
+        finish(nc.gpsimd, 0, 0, T)
+        scale(2, 0, T)
+        finish(nc.vector, 1, 0, T)
+        finish(nc.vector, 2, 0, T)
+        scale(3, 0, half)
+        scale(3, half, half)
+        finish(nc.vector, 3, 0, half)
+        finish(nc.vector, 3, half, half)

from contextlib import ExitStack

import concourse.mybir as mybir
from concourse.masks import make_identity

K, R, N, T = 1024, 512, 512, 512
FLOPS = 2 * T * (K * R + K * N + R * N)

F32 = mybir.dt.float32
BF16 = mybir.dt.bfloat16
I32 = mybir.dt.int32
U32 = mybir.dt.uint32
U8 = mybir.dt.uint8
FP8X4 = mybir.dt.float8_e4m3fn_x4
ADD = mybir.AluOpType.add
MULT = mybir.AluOpType.mult

P = 128
PACK = 4
K_PASS = P * PACK
PASSES = K // K_PASS
TILES = 4
LINE = 4


def tile_mix_cross_none_kernel(tc, x, wb_words, wb_scales, dn, upw, x0, b, xr, out):
    nc = tc.nc

    with ExitStack() as ctx:
        sb = ctx.enter_context(tc.tile_pool(name="sb", bufs=1))
        ps = ctx.enter_context(tc.psum_pool(name="ps", bufs=1))
        ctx.enter_context(tc.manual_schedule())

        def sbuf(name, shape, dtype):
            return sb.tile(shape, dtype, name=name, align_bytes=64)

        def operand(name):
            return sbuf(name + "_codes", [P, 512], U32), sbuf(name + "_scales", [P, 512], U8)

        def load_rows(name, rows):
            raw = sbuf(name, [P, PACK, rows.shape[1]], F32)
            nc.sync.dma_start(out=raw[:], in_=rows.rearrange("(p k) w -> p k w", k=PACK))
            return raw

        def load_tile(name, src, c, t0, width):
            t = sbuf(name, [P, width], F32)
            nc.sync.dma_start(out=t[:], in_=src[c * P : (c + 1) * P, t0 : t0 + width])
            return t

        def load_wb(a):
            words = sbuf("wb_codes%d" % a, [P, N], U32)
            nc.sync.dma_start(out=words[:].bitcast(I32), in_=wb_words[a].rearrange("p n i -> p (n i)").bitcast(I32))
            return words

        def copy_on(engine, dst, src):
            if engine == "vector":
                nc.vector.tensor_copy(out=dst, in_=src)
            else:
                nc.scalar.copy(out=dst, in_=src)

        def interleave(engine, name, raw, lo, width):
            grouped = sbuf(name, [P, width, PACK], BF16)
            copy_on(
                engine,
                grouped[:].rearrange("p (c i) k -> p c k i", i=LINE),
                raw[:, :, lo : lo + width].rearrange("p k (c i) -> p c k i", i=LINE),
            )
            return grouped

        def interleave_dn(engine, name, raw, j0):
            grouped = sbuf(name, [P, 2 * P, PACK], BF16)
            copy_on(
                engine,
                grouped[:].rearrange("p (j m) k -> p m k j", j=2),
                raw[:].rearrange("p k (m j) -> p m k j", j=PACK)[:, :, :, j0 : j0 + 2],
            )
            return grouped

        def quantize(dst, lo, grouped):
            codes, scales = dst
            width = grouped.shape[1]
            nc.vector.quantize_mx(
                out=codes[:, lo : lo + width].bitcast(FP8X4),
                scales=scales[:, lo : lo + width],
                in_=grouped[:].rearrange("p w k -> p (w k)"),
            )

        def mx(acc, lhs, lhs_lo, rhs, rhs_lo, width, start, stop):
            nc.tensor.matmul_mx(
                out=acc,
                lhsT=lhs[0][:, lhs_lo : lhs_lo + P].bitcast(FP8X4),
                lhsT_scale=lhs[1][:, lhs_lo : lhs_lo + P],
                rhs=rhs[0][:, rhs_lo : rhs_lo + width].bitcast(FP8X4),
                rhs_scale=rhs[1][:, rhs_lo : rhs_lo + width],
                start=start,
                stop=stop,
            )

        half = T // 2
        dn_raw0 = load_rows("dn_raw0", dn[0:K_PASS, :])
        b_rows = sbuf("b_rows", [P, P], F32)
        nc.vector.memset(b_rows[:], 0.0)
        nc.sync.dma_start(out=b_rows[0:TILES, :], in_=b.rearrange("(c p) -> c p", p=P))
        dn_raw1 = load_rows("dn_raw1", dn[K_PASS:K, :])
        x_raw0 = load_rows("x_raw0", x[0:K_PASS, :])
        x_raw1 = load_rows("x_raw1", x[K_PASS:K, :])
        wb_plane = sbuf("wb_plane", [P, N], U8)
        nc.vector.memset(wb_plane[:].bitcast(I32), 0)
        scale_words = wb_scales.bitcast(I32)
        for q in range(4):
            nc.sync.dma_start(
                out=wb_plane[32 * q : 32 * q + 8, :].bitcast(I32),
                in_=scale_words[:, 4 * q : 4 * q + 4, :],
            )
        up_raw = load_rows("up_raw", upw)
        wb_codes0 = load_wb(0)
        wb_codes1 = load_wb(1)
        x0_t = [None] * TILES
        xr_t = [None] * TILES
        for name, c in (("x0", 0), ("x0", 1), ("xr", 0), ("x0", 2), ("xr", 1), ("xr", 2), ("x0", 3), ("xr", 3)):
            if name == "x0":
                x0_t[c] = load_tile("x0_%d" % c, x0, c, 0, T)
            else:
                xr_t[c] = load_tile("xr_%d" % c, xr, c, 0, T)

        wb = [(wb_codes0, wb_plane[0:P, :]), (wb_codes1, wb_plane[4:P, :])]
        ident = sbuf("ident", [P, P], F32)
        make_identity(nc, ident[:])

        hs = [ps.tile([P, PACK, P], F32, name="hs%d" % q) for q in range(TILES)]
        y = [ps.tile([P, T], F32, name="y%d" % c) for c in range(TILES)]

        dn_q = [operand("dn0"), operand("dn1")]
        x_q = [operand("x0q"), operand("x1q")]
        up_q = operand("up")
        h_q = operand("h")

        def prepare_dn(a, raw):
            lo = interleave_dn("vector", "dn_lo%d" % a, raw, 0)
            hi = interleave_dn("scalar", "dn_hi%d" % a, raw, 2)
            quantize(dn_q[a], 0, lo)
            quantize(dn_q[a], 2 * P, hi)

        def prepare_x(a, raw):
            groups = [
                interleave("vector" if q % 2 == 0 else "scalar", "xg%d_%d" % (a, q), raw, q * P, P) for q in range(TILES)
            ]
            for q in range(TILES):
                quantize(x_q[a], q * P, groups[q])

        def hs_pass(a, q):
            for j in range(PACK):
                mx(hs[q][:, j, :], dn_q[a], j * P, x_q[a], q * P, P,
                   start=(a == 0 and j == 0), stop=(a == PASSES - 1 and j == PACK - 1))

        prepare_dn(0, dn_raw0)
        nc.tensor.transpose(y[TILES - 1][:, 0:P], b_rows[:], ident[:])
        b_cols = sbuf("b_cols", [P, TILES], F32)
        nc.scalar.copy(out=b_cols[:], in_=y[TILES - 1][:, 0:TILES])
        prepare_dn(1, dn_raw1)
        for a, raw in enumerate((x_raw0, x_raw1)):
            prepare_x(a, raw)
            for q in range(TILES):
                hs_pass(a, q)

        h01 = sbuf("h01", [P, half, PACK], BF16)
        h2 = sbuf("h2", [P, P, PACK], BF16)
        h3 = sbuf("h3", [P, P, PACK], BF16)

        def drain_h(engine, q, dst):
            copy_on(engine, dst, hs[q][:].rearrange("p j t -> p t j"))

        drain_h("scalar", 0, h01[:, 0:P, :])
        drain_h("vector", 1, h01[:, P:half, :])
        drain_h("scalar", 2, h2[:])
        drain_h("scalar", 3, h3[:])

        def base_pass(a, c):
            mx(y[c][:], wb[a], c * P, x_q[a], 0, T, start=(a == 0), stop=False)

        def branch_pass(c, t0, width):
            mx(y[c][:, t0 : t0 + width], up_q, c * P, h_q, t0, width, start=False, stop=(t0 + width == T))

        up_g0 = interleave("vector", "up_g0", up_raw, 0, P)
        quantize(h_q, 0, h01)
        quantize(up_q, 0, up_g0)
        up_g1 = interleave("vector", "up_g1", up_raw, P, P)
        quantize(h_q, 2 * P, h2)
        quantize(h_q, 3 * P, h3)
        up_g2 = interleave("scalar", "up_g2", up_raw, 2 * P, P)
        up_g3 = interleave("scalar", "up_g3", up_raw, 3 * P, P)
        quantize(up_q, P, up_g1)
        quantize(up_q, 2 * P, up_g2)

        z = sbuf("z", [P, TILES, T], F32)

        def scale(c, t0, width):
            cols = slice(t0, t0 + width)
            nc.vector.scalar_tensor_tensor(
                out=z[:, c, cols], in0=y[c][:, cols], scalar=b_cols[:, c : c + 1], in1=x0_t[c][:, cols], op0=ADD, op1=MULT
            )

        def finish(engine, c, t0, width):
            cols = slice(t0, t0 + width)
            engine.tensor_tensor(out=z[:, c, cols], in0=z[:, c, cols], in1=xr_t[c][:, cols], op=ADD)
            nc.sync.dma_start(out=out[c * P : (c + 1) * P, cols], in_=z[:, c, cols])

        base_pass(0, 0)
        base_pass(0, 1)
        base_pass(1, 0)
        branch_pass(0, 0, half)
        branch_pass(0, half, half)
        base_pass(1, 1)
        branch_pass(1, 0, T)
        base_pass(0, 2)
        base_pass(1, 2)
        branch_pass(2, 0, T)
        scale(0, 0, T)
        quantize(up_q, 3 * P, up_g3)
        base_pass(0, 3)
        base_pass(1, 3)
        branch_pass(3, 0, T)
        scale(1, 0, T)
        finish(nc.gpsimd, 0, 0, T)
        scale(2, 0, T)
        finish(nc.vector, 1, 0, T)
        finish(nc.vector, 2, 0, T)
        scale(3, 0, half)
        scale(3, half, half)
        finish(nc.vector, 3, 0, half)
        finish(nc.vector, 3, half, half)
